import numpy as np
import ml_dtypes


def mxq(x, axis, fmt="e4m3"):
    dtype, down = {"e4m3": (ml_dtypes.float8_e4m3fn, 7), "e5m2": (ml_dtypes.float8_e5m2, 14)}[fmt]
    v = np.moveaxis(np.asarray(x, np.float32).astype(ml_dtypes.bfloat16).astype(np.float64), axis, -1)
    blocks = v.reshape(v.shape[:-1] + (-1, 32))
    amax = np.abs(blocks).max(-1, keepdims=True)
    byte = np.maximum(np.where(amax > 0, np.frexp(amax)[1] - 1 + 127, 0) - down, 1)
    scale = np.exp2(byte - 127.0)
    codes = (blocks / scale).astype(np.float32).astype(dtype).astype(np.float64)
    return np.moveaxis((codes * scale).reshape(v.shape), -1, axis)


WIDE = False


def mx_kscale(k):
    if not WIDE:
        return np.ones(k)
    levels = np.array([10, -10, 5, -5, 0])
    if k % 512:
        return np.exp2(np.random.permutation(np.resize(levels, k // 32))).repeat(32)
    a = np.empty((k // 512, 16))
    for p in range(k // 512):
        a[p, :8] = np.random.permutation(np.resize(levels, 8))
        for g in range(8):
            far = levels[np.abs(levels - a[p, g]) >= 10]
            a[p, g + 8] = far[np.random.randint(len(far))]
    return np.exp2(a.ravel()).repeat(32)


def f64(x):
    return np.asarray(x).astype(np.float64)


def striped(idx):
    return np.tile(idx.reshape(-1, 16).T, (8, 1)).astype(np.uint16)


def unstriped(offs):
    return offs[:16].T.reshape(-1).astype(np.int64)


def striped8(idx):
    return np.concatenate([x.reshape(-1, 16).T for x in idx]).astype(np.uint16)


def runs(offs, k):
    lists = np.stack([offs[16 * r : 16 * r + 16].T.reshape(-1) for r in range(8)]).astype(np.int64)
    return lists[np.arange(k) % 512 // 64]


def pack_weight(w):
    k, n = w.shape
    w = f64(np.asarray(w, np.float32).astype(ml_dtypes.bfloat16)).reshape(k // 32, 32, n)
    amax = np.abs(w).max(1)
    byte = np.clip(np.where(amax > 0, np.frexp(amax)[1] - 1 + 127 - 7, 1), 1, 254)
    scaled = (w * np.exp2(127.0 - byte)[:, None, :]).reshape(k, n).astype(np.float32)
    words = np.ascontiguousarray(scaled.reshape(k // 512, 128, 4, n).transpose(0, 1, 3, 2)).astype(ml_dtypes.float8_e4m3fn).view(np.uint8)
    return words, np.ascontiguousarray(byte.astype(np.uint8).reshape(k // 512, 16, n))


def unpack_weight(words, scales):
    g, p, n, _ = words.shape
    vals = np.ascontiguousarray(words).view(ml_dtypes.float8_e4m3fn).astype(np.float64) * np.repeat(np.exp2(scales.astype(np.float64) - 127.0), 8, axis=1)[..., None]
    return vals.transpose(0, 1, 3, 2).reshape(g * 512, n)


def sigmoid(v):
    return 1.0 / (1.0 + np.exp(-np.maximum(v, -700.0)))


K, T, S, N, H, U = 512, 2048, 512, 512, 512, 1024


def setup_inputs():
    n = np.random.standard_normal
    s = mx_kscale(K)[:, None]
    u = mx_kscale(H)
    packed_xT = pack_weight(n((K, T)) * s)
    return {
        "x_words": packed_xT[0],
        "x_scales": packed_xT[1],
        "w1": (n((K, H)) / np.sqrt(K) / s).astype(np.float32),
        "w2": (n((K, H)) / np.sqrt(K) / s).astype(np.float32),
        "gn": (np.random.uniform(0.5, 1.5, (H, 1)) * u[:, None]).astype(np.float32),
        "w3": (n((H, N)) / np.sqrt(H) / u[:, None]).astype(np.float32),
        "mem": n((N, U)).astype(np.float32),
        "offs": striped(np.random.permutation(T)[:S]),
        "hz": striped8(np.random.randint(0, T, (8, S))),
        "n1": striped(np.random.permutation(S)),
        "n2": striped(np.random.permutation(S)),
        "n3": striped(np.random.permutation(U)[:S]),
    }


def reference(x_words, x_scales, w1, w2, gn, w3, mem, offs, hz, n1, n2, n3):
    old = f64(mem)[:, unstriped(n3)]
    xq = unpack_weight(x_words, x_scales)[:, unstriped(offs)]
    y = mxq(f64(w1), 0, "e4m3").T @ xq
    x_hz = unpack_weight(x_words, x_scales)[np.arange(K)[:, None], runs(hz, K)]
    d = mxq(f64(w2), 0, "e4m3").T @ x_hz
    z = f64(gn) * (0.75 * (y * d[:, unstriped(n2)] - (y[:, unstriped(n1)] * d)))
    h = mxq(f64(w3), 0, "e4m3").T @ mxq(z, 0, "e4m3")
    nw = old + sigmoid(h) * (h - old)
    out = f64(mem).copy()
    out[:, unstriped(n3)] = nw
    return out

@@ -1,0 +1,196 @@
+from contextlib import ExitStack
+
+import concourse.mybir as mybir
+
+K, T, S, N, H, U = 512, 2048, 512, 512, 512, 1024
+FLOPS = 2 * S * (K * H + K * H + H * N)
+
+F32 = mybir.dt.float32
+BF16 = mybir.dt.bfloat16
+I32 = mybir.dt.int32
+U32 = mybir.dt.uint32
+U16 = mybir.dt.uint16
+U8 = mybir.dt.uint8
+FP8X4 = mybir.dt.float8_e4m3fn_x4
+ALU = mybir.AluOpType
+ACT = mybir.ActivationFunctionType
+
+P = 128
+PACK = 4
+PIECES = ((0, 256), (256, 512))
+
+
+def tile_picked_twhcrossbpaget_none_p_kernel(tc, x_words, x_scales, w1, w2, gn, w3, mem, offs, hz, n1, n2, n3, out):
+    nc = tc.nc
+    with ExitStack() as ctx:
+        lists = ctx.enter_context(tc.tile_pool(name="lists", bufs=1))
+        keep = ctx.enter_context(tc.tile_pool(name="keep", bufs=1))
+        shared = ctx.enter_context(tc.tile_pool(name="shared", bufs=1))
+        psum = ctx.enter_context(tc.psum_pool(name="psum", bufs=8))
+
+        def load_list(src, name):
+            tile = lists.tile([P, S // 16], U16, name=name)
+            nc.sync.dma_start(tile[:], src)
+            return tile
+
+        def entries(tile, lo, hi):
+            return tile[:, lo // 16 : hi // 16]
+
+        l_offs = load_list(offs, "l_offs")
+        l_hz = load_list(hz, "l_hz")
+        scale_table = keep.tile([P, T], U8, name="scale_table", align_bytes=64)
+        nc.vector.memset(scale_table[:].bitcast(I32), 0)
+        nc.scalar.dma_start(scale_table[0:P:8, :].bitcast(I32), x_scales[0].bitcast(I32))
+        word_table = shared.tile([P, T], U32, name="word_table", offset=0)
+        nc.sync.dma_start(word_table[:].bitcast(I32), x_words[0].rearrange("p n t -> p (n t)").bitcast(I32))
+        l_n1 = load_list(n1, "l_n1")
+        l_n3 = load_list(n3, "l_n3")
+        gain = keep.tile([P, PACK], F32, name="gain")
+        nc.sync.dma_start(gain[:], gn.rearrange("(p t) o -> p (t o)", t=PACK))
+        l_n2 = load_list(n2, "l_n2")
+
+        def load_weight(w, name, tag):
+            raw = keep.tile([P, PACK, 512], F32, name=name, tag=tag)
+            nc.sync.dma_start(raw[:], w.rearrange("(p j) c -> p j c", j=PACK))
+            return raw
+
+        def load_page(m, tile):
+            nc.sync.dma_start(tile[:], mem[m * P : (m + 1) * P, :])
+            return tile
+
+        w1_raw = load_weight(w1, "w1_raw", "raw_a")
+        pages = [load_page(m, keep.tile([P, U], F32, name=f"page{m}")) for m in range(2)]
+        w2_raw = load_weight(w2, "w2_raw", "raw_b")
+
+        picked_scales = keep.tile([P, 2 * S], U8, name="picked_scales", align_bytes=64)
+        nc.vector.tensor_copy(picked_scales[:, 0:S], scale_table[:].indirect(l_offs[:]))
+        nc.vector.tensor_copy(picked_scales[:, S : 2 * S], scale_table[:].indirect(l_hz[:]))
+        placed_scales = keep.tile([P, 2 * S], U8, name="placed_scales", align_bytes=64)
+        nc.vector.tensor_copy(placed_scales[:].bitcast(I32), picked_scales[:].bitcast(I32))
+        for r in range(1, 4):
+            nc.scalar.dma_start(placed_scales[r:P:32, :].bitcast(I32), picked_scales[8 * r : P : 32, :].bitcast(I32))
+        words_offs = keep.tile([P, S], U32, name="words_offs", align_bytes=64)
+        nc.vector.tensor_copy(words_offs[:], word_table[:].indirect(l_offs[:]))
+        words_hz = keep.tile([P, S], U32, name="words_hz", align_bytes=64)
+        nc.vector.tensor_copy(words_hz[:], word_table[:].indirect(l_hz[:]))
+
+        for m in range(2, 4):
+            pages.append(load_page(m, shared.tile([P, U], F32, name=f"page{m}", offset=(m - 2) * U * 4)))
+
+        def quantise(values, name):
+            width = values.shape[1] // PACK
+            codes = keep.tile([P, width], U32, name=name + "_codes", align_bytes=64)
+            scales = keep.tile([P, width], U8, name=name + "_scales", align_bytes=64)
+            nc.vector.quantize_mx(out=codes[:].bitcast(FP8X4), scales=scales[:], in_=values)
+            return codes, scales
+
+        def first_product(raw, words, scale_cols, name, leave):
+            for half in range(2):
+                rounded = keep.tile([P, 2 * P * PACK], BF16, name=f"{name}_bf{half}", align_bytes=64)
+                nc.vector.tensor_copy(
+                    rounded[:].rearrange("p (t m j) -> p m t j", t=2, j=PACK),
+                    raw[:].rearrange("p j (m t) -> p m t j", t=PACK)[:, :, 2 * half : 2 * half + 2, :],
+                )
+                codes, scales = quantise(rounded[:], f"{name}_q{half}")
+                for u in range(2):
+                    acc = psum.tile([P, S], F32, name="acc")
+                    nc.tensor.matmul_mx(
+                        out=acc[:],
+                        lhsT=codes[:, u * P : (u + 1) * P].bitcast(FP8X4),
+                        lhsT_scale=scales[:, u * P : (u + 1) * P],
+                        rhs=words[:].bitcast(FP8X4),
+                        rhs_scale=placed_scales[:, scale_cols],
+                        start=True,
+                        stop=True,
+                    )
+                    leave(2 * half + u, acc)
+
+        old = []
+
+        def fetch_old(m, tag):
+            tile = keep.tile([P, S], F32, name=f"old{m}", tag=tag)
+            nc.scalar.activation(tile[:], pages[m][:].indirect(l_n3[:]), ACT.Copy)
+            old.append(tile)
+
+        fetch_old(0, "old0")
+        fetch_old(1, "old1")
+
+        y_rows, d_rows, d_banks = [], [], []
+        y_picked = [keep.tile([P, PACK, hi - lo], F32, name=f"y_picked{i}") for i, (lo, hi) in enumerate(PIECES)]
+        d_picked = [keep.tile([P, PACK, hi - lo], F32, name=f"d_picked{i}") for i, (lo, hi) in enumerate(PIECES)]
+
+        def leave_y(t, acc):
+            row = keep.tile([P, S], F32, name=f"y{t}")
+            nc.vector.tensor_scalar(row[:], acc[:], gain[:, t : t + 1], None, ALU.mult)
+            y_rows.append(row)
+            for i, (lo, hi) in enumerate(PIECES):
+                nc.scalar.activation(y_picked[i][:, t, :], row[:].indirect(entries(l_n1, lo, hi)), ACT.Copy)
+
+        def leave_d(t, acc):
+            row = keep.tile([P, S], F32, name=f"d{t}", tag=f"d{t}")
+            nc.vector.tensor_scalar(row[:], acc[:], 0.75, None, ALU.mult)
+            d_rows.append(row)
+            d_banks.append(acc)
+
+        first_product(w1_raw, words_offs, slice(0, S), "w1", leave_y)
+        w3_raw = load_weight(w3, "w3_raw", "raw_a")
+        first_product(w2_raw, words_hz, slice(S, 2 * S), "w2", leave_d)
+        for i, (lo, hi) in enumerate(PIECES):
+            for t in range(PACK):
+                nc.scalar.activation(d_picked[i][:, t, :], d_rows[t][:].indirect(entries(l_n2, lo, hi)), ACT.Copy)
+        fetch_old(2, "d2")
+        fetch_old(3, "d3")
+
+        w3_bf = keep.tile([P, N * PACK], BF16, name="w3_bf", align_bytes=64)
+        nc.vector.tensor_copy(w3_bf[:].rearrange("p (c j) -> p c j", j=PACK), w3_raw[:].rearrange("p j c -> p c j"))
+        w3_codes, w3_scales = quantise(w3_bf[:], "w3_q")
+
+        def make_z(i):
+            lo, hi = PIECES[i]
+            width = hi - lo
+            first = keep.tile([P, PACK, width], F32, name=f"first{i}")
+            second = keep.tile([P, PACK, width], F32, name=f"second{i}")
+            for t in range(PACK):
+                nc.vector.scalar_tensor_tensor(
+                    second[:, t, :], d_banks[t][:, lo:hi], 0.75, y_picked[i][:, t, :], ALU.mult, ALU.mult
+                )
+            for t in range(PACK):
+                nc.vector.tensor_tensor(first[:, t, :], y_rows[t][:, lo:hi], d_picked[i][:, t, :], ALU.mult)
+            z_bf = keep.tile([P, width * PACK], BF16, name=f"z_bf{i}", align_bytes=64)
+            nc.vector.tensor_tensor(
+                z_bf[:].rearrange("p (c e t) -> p c t e", e=4, t=PACK),
+                first[:].rearrange("p t (c e) -> p c t e", e=4),
+                second[:].rearrange("p t (c e) -> p c t e", e=4),
+                ALU.subtract,
+            )
+            return quantise(z_bf[:], f"z_q{i}")
+
+        def write_piece(i, z_codes, z_scales):
+            lo, hi = PIECES[i]
+            width = hi - lo
+            for m in range(4):
+                acc = psum.tile([P, S], F32, name="acc")
+                h = acc[:, 0:width]
+                nc.tensor.matmul_mx(
+                    out=h,
+                    lhsT=w3_codes[:, m * P : (m + 1) * P].bitcast(FP8X4),
+                    lhsT_scale=w3_scales[:, m * P : (m + 1) * P],
+                    rhs=z_codes[:].bitcast(FP8X4),
+                    rhs_scale=z_scales[:],
+                    start=True,
+                    stop=True,
+                )
+                half_tanh = keep.tile([P, width], F32, name=f"tanh{i}_{m}")
+                nc.scalar.activation(half_tanh[:], h, ACT.Tanh, scale=0.5)
+                gap = keep.tile([P, width], F32, name=f"gap{i}_{m}")
+                nc.vector.tensor_tensor(gap[:], h, old[m][:, lo:hi], ALU.subtract)
+                step = keep.tile([P, width], F32, name=f"step{i}_{m}")
+                nc.vector.scalar_tensor_tensor(step[:], half_tanh[:], 1.0, gap[:], ALU.add, ALU.mult)
+                new = keep.tile([P, width], F32, name=f"new{i}_{m}")
+                nc.vector.scalar_tensor_tensor(new[:], step[:], 0.5, old[m][:, lo:hi], ALU.mult, ALU.add)
+                nc.scalar.activation(pages[m][:].indirect(entries(l_n3, lo, hi)), new[:], ACT.Copy)
+                if hi == S:
+                    nc.sync.dma_start(out[m * P : (m + 1) * P, :], pages[m][:])
+
+        for i in range(len(PIECES)):
+            write_piece(i, *make_z(i))

@@ -36,21 +36,23 @@ def tile_picked_twhcrossbpaget_none_p_kernel(tc, x_words, x_scales, w1, w2, gn, 
         def entries(tile, lo, hi):
             return tile[:, lo // 16 : hi // 16]
 
+        gn_rows = keep.tile([P, PACK], F32, name="gn_rows")
+        nc.sync.dma_start(gn_rows[:], gn.rearrange("(p t) o -> p (t o)", t=PACK))
+        gain = keep.tile([P, PACK], F32, name="gain")
+        nc.scalar.activation(gain[:], gn_rows[:], ACT.Copy, scale=0.75)
         l_offs = load_list(offs, "l_offs")
         l_hz = load_list(hz, "l_hz")
-        scale_table = keep.tile([P, T], U8, name="scale_table", align_bytes=64)
+        l_n3 = load_list(n3, "l_n3")
+        l_n1 = load_list(n1, "l_n1")
+        l_n2 = load_list(n2, "l_n2")
+        scale_table = shared.tile([P, T], U8, name="scale_table", align_bytes=64, offset=16384 + 3072)
         nc.vector.memset(scale_table[:].bitcast(I32), 0)
-        nc.scalar.dma_start(scale_table[0:P:8, :].bitcast(I32), x_scales[0].bitcast(I32))
+        nc.sync.dma_start(scale_table[0:P:8, :].bitcast(I32), x_scales[0].bitcast(I32))
         word_table = shared.tile([P, T], U32, name="word_table", offset=0)
         nc.sync.dma_start(word_table[:].bitcast(I32), x_words[0].rearrange("p n t -> p (n t)").bitcast(I32))
-        l_n1 = load_list(n1, "l_n1")
-        l_n3 = load_list(n3, "l_n3")
-        gain = keep.tile([P, PACK], F32, name="gain")
-        nc.sync.dma_start(gain[:], gn.rearrange("(p t) o -> p (t o)", t=PACK))
-        l_n2 = load_list(n2, "l_n2")
 
-        def load_weight(w, name, tag):
-            raw = keep.tile([P, PACK, 512], F32, name=name, tag=tag)
+        def load_weight(w, name, offset):
+            raw = shared.tile([P, PACK, 512], F32, name=name, offset=offset)
             nc.sync.dma_start(raw[:], w.rearrange("(p j) c -> p j c", j=PACK))
             return raw
 
@@ -58,24 +60,23 @@ def tile_picked_twhcrossbpaget_none_p_kernel(tc, x_words, x_scales, w1, w2, gn, 
             nc.sync.dma_start(tile[:], mem[m * P : (m + 1) * P, :])
             return tile
 
-        w1_raw = load_weight(w1, "w1_raw", "raw_a")
-        pages = [load_page(m, keep.tile([P, U], F32, name=f"page{m}")) for m in range(2)]
-        w2_raw = load_weight(w2, "w2_raw", "raw_b")
+        w1_raw = load_weight(w1, "w1_raw", 8192)
+        pages = [load_page(0, keep.tile([P, U], F32, name="page0"))]
 
         picked_scales = keep.tile([P, 2 * S], U8, name="picked_scales", align_bytes=64)
         nc.vector.tensor_copy(picked_scales[:, 0:S], scale_table[:].indirect(l_offs[:]))
         nc.vector.tensor_copy(picked_scales[:, S : 2 * S], scale_table[:].indirect(l_hz[:]))
         placed_scales = keep.tile([P, 2 * S], U8, name="placed_scales", align_bytes=64)
-        nc.vector.tensor_copy(placed_scales[:].bitcast(I32), picked_scales[:].bitcast(I32))
-        for r in range(1, 4):
-            nc.scalar.dma_start(placed_scales[r:P:32, :].bitcast(I32), picked_scales[8 * r : P : 32, :].bitcast(I32))
+        nc.vector.memset(placed_scales[:].bitcast(I32), 0)
+        for r in range(4):
+            nc.sync.dma_start(placed_scales[r:P:32, :].bitcast(I32), picked_scales[8 * r : P : 32, :].bitcast(I32))
+        pages.append(load_page(1, shared.tile([P, U], F32, name="page1", offset=16384)))
+        w2_raw = load_weight(w2, "w2_raw", 20480)
         words_offs = keep.tile([P, S], U32, name="words_offs", align_bytes=64)
         nc.vector.tensor_copy(words_offs[:], word_table[:].indirect(l_offs[:]))
         words_hz = keep.tile([P, S], U32, name="words_hz", align_bytes=64)
         nc.vector.tensor_copy(words_hz[:], word_table[:].indirect(l_hz[:]))
-
-        for m in range(2, 4):
-            pages.append(load_page(m, shared.tile([P, U], F32, name=f"page{m}", offset=(m - 2) * U * 4)))
+        w3_raw = load_weight(w3, "w3_raw", 0)
 
         def quantise(values, name):
             width = values.shape[1] // PACK
@@ -84,10 +85,10 @@ def tile_picked_twhcrossbpaget_none_p_kernel(tc, x_words, x_scales, w1, w2, gn, 
             nc.vector.quantize_mx(out=codes[:].bitcast(FP8X4), scales=scales[:], in_=values)
             return codes, scales
 
-        def first_product(raw, words, scale_cols, name, leave):
+        def first_product(raw, words, scale_cols, name, leave, casts):
             for half in range(2):
                 rounded = keep.tile([P, 2 * P * PACK], BF16, name=f"{name}_bf{half}", align_bytes=64)
-                nc.vector.tensor_copy(
+                casts[half](
                     rounded[:].rearrange("p (t m j) -> p m t j", t=2, j=PACK),
                     raw[:].rearrange("p j (m t) -> p m t j", t=PACK)[:, :, 2 * half : 2 * half + 2, :],
                 )
@@ -112,12 +113,9 @@ def tile_picked_twhcrossbpaget_none_p_kernel(tc, x_words, x_scales, w1, w2, gn, 
             nc.scalar.activation(tile[:], pages[m][:].indirect(l_n3[:]), ACT.Copy)
             old.append(tile)
 
-        fetch_old(0, "old0")
-        fetch_old(1, "old1")
-
         y_rows, d_rows, d_banks = [], [], []
-        y_picked = [keep.tile([P, PACK, hi - lo], F32, name=f"y_picked{i}") for i, (lo, hi) in enumerate(PIECES)]
-        d_picked = [keep.tile([P, PACK, hi - lo], F32, name=f"d_picked{i}") for i, (lo, hi) in enumerate(PIECES)]
+        y_picked = [keep.tile([P, PACK, hi - lo], F32, name=f"y_picked{i}", tag=f"picked{i}") for i, (lo, hi) in enumerate(PIECES)]
+        d_picked = []
 
         def leave_y(t, acc):
             row = keep.tile([P, S], F32, name=f"y{t}")
@@ -128,32 +126,44 @@ def tile_picked_twhcrossbpaget_none_p_kernel(tc, x_words, x_scales, w1, w2, gn, 
 
         def leave_d(t, acc):
             row = keep.tile([P, S], F32, name=f"d{t}", tag=f"d{t}")
-            nc.vector.tensor_scalar(row[:], acc[:], 0.75, None, ALU.mult)
+            nc.vector.tensor_copy(row[:], acc[:])
             d_rows.append(row)
             d_banks.append(acc)
 
-        first_product(w1_raw, words_offs, slice(0, S), "w1", leave_y)
-        w3_raw = load_weight(w3, "w3_raw", "raw_a")
-        first_product(w2_raw, words_hz, slice(S, 2 * S), "w2", leave_d)
-        for i, (lo, hi) in enumerate(PIECES):
+        first_product(w1_raw, words_offs, slice(0, S), "w1", leave_y, (nc.vector.tensor_copy, nc.scalar.copy))
+        fetch_old(0, "old0")
+        fetch_old(1, "old1")
+        for m in range(2, 4):
+            pages.append(load_page(m, shared.tile([P, U], F32, name=f"page{m}", offset=8192 + (m - 2) * U * 4)))
+        first_product(w2_raw, words_hz, slice(S, 2 * S), "w2", leave_d, (nc.vector.tensor_copy, nc.vector.tensor_copy))
+
+        def fetch_d(i, tag):
+            lo, hi = PIECES[i]
+            tile = keep.tile([P, PACK, hi - lo], F32, name=f"d_picked{i}", tag=tag)
             for t in range(PACK):
-                nc.scalar.activation(d_picked[i][:, t, :], d_rows[t][:].indirect(entries(l_n2, lo, hi)), ACT.Copy)
-        fetch_old(2, "d2")
-        fetch_old(3, "d3")
+                nc.scalar.activation(tile[:, t, :], d_rows[t][:].indirect(entries(l_n2, lo, hi)), ACT.Copy)
+            d_picked.append(tile)
 
-        w3_bf = keep.tile([P, N * PACK], BF16, name="w3_bf", align_bytes=64)
-        nc.vector.tensor_copy(w3_bf[:].rearrange("p (c j) -> p c j", j=PACK), w3_raw[:].rearrange("p j c -> p c j"))
-        w3_codes, w3_scales = quantise(w3_bf[:], "w3_q")
+        def quantise_w3(half):
+            cols = slice(half * 2 * P, (half + 1) * 2 * P)
+            rounded = keep.tile([P, 2 * P * PACK], BF16, name=f"w3_bf{half}", align_bytes=64)
+            nc.vector.tensor_copy(
+                rounded[:].rearrange("p (c j) -> p c j", j=PACK), w3_raw[:, :, cols].rearrange("p j c -> p c j")
+            )
+            return quantise(rounded[:], f"w3_q{half}")
 
-        def make_z(i):
+        def second_term(i):
             lo, hi = PIECES[i]
             width = hi - lo
-            first = keep.tile([P, PACK, width], F32, name=f"first{i}")
-            second = keep.tile([P, PACK, width], F32, name=f"second{i}")
+            second = keep.tile([P, PACK, width], F32, name=f"second{i}", tag=f"product{(i + 1) % 2}")
             for t in range(PACK):
-                nc.vector.scalar_tensor_tensor(
-                    second[:, t, :], d_banks[t][:, lo:hi], 0.75, y_picked[i][:, t, :], ALU.mult, ALU.mult
-                )
+                nc.vector.tensor_tensor(second[:, t, :], d_banks[t][:, lo:hi], y_picked[i][:, t, :], ALU.mult)
+            return second
+
+        def make_z(i, second):
+            lo, hi = PIECES[i]
+            width = hi - lo
+            first = keep.tile([P, PACK, width], F32, name=f"first{i}", tag=f"product{i % 2}")
             for t in range(PACK):
                 nc.vector.tensor_tensor(first[:, t, :], y_rows[t][:, lo:hi], d_picked[i][:, t, :], ALU.mult)
             z_bf = keep.tile([P, width * PACK], BF16, name=f"z_bf{i}", align_bytes=64)
@@ -173,17 +183,20 @@ def tile_picked_twhcrossbpaget_none_p_kernel(tc, x_words, x_scales, w1, w2, gn, 
                 h = acc[:, 0:width]
                 nc.tensor.matmul_mx(
                     out=h,
-                    lhsT=w3_codes[:, m * P : (m + 1) * P].bitcast(FP8X4),
-                    lhsT_scale=w3_scales[:, m * P : (m + 1) * P],
+                    lhsT=w3_q[m // 2][0][:, m % 2 * P : (m % 2 + 1) * P].bitcast(FP8X4),
+                    lhsT_scale=w3_q[m // 2][1][:, m % 2 * P : (m % 2 + 1) * P],
                     rhs=z_codes[:].bitcast(FP8X4),
                     rhs_scale=z_scales[:],
                     start=True,
                     stop=True,
                 )
-                half_tanh = keep.tile([P, width], F32, name=f"tanh{i}_{m}")
-                nc.scalar.activation(half_tanh[:], h, ACT.Tanh, scale=0.5)
                 gap = keep.tile([P, width], F32, name=f"gap{i}_{m}")
-                nc.vector.tensor_tensor(gap[:], h, old[m][:, lo:hi], ALU.subtract)
+                half_tanh = keep.tile([P, width], F32, name=f"tanh{i}_{m}")
+                if m < 2:
+                    nc.vector.tensor_tensor(gap[:], h, old[m][:, lo:hi], ALU.subtract)
+                nc.scalar.activation(half_tanh[:], h, ACT.Tanh, scale=0.5)
+                if m >= 2:
+                    nc.vector.tensor_tensor(gap[:], h, old[m][:, lo:hi], ALU.subtract)
                 step = keep.tile([P, width], F32, name=f"step{i}_{m}")
                 nc.vector.scalar_tensor_tensor(step[:], half_tanh[:], 1.0, gap[:], ALU.add, ALU.mult)
                 new = keep.tile([P, width], F32, name=f"new{i}_{m}")
@@ -192,5 +205,12 @@ def tile_picked_twhcrossbpaget_none_p_kernel(tc, x_words, x_scales, w1, w2, gn, 
                 if hi == S:
                     nc.sync.dma_start(out[m * P : (m + 1) * P, :], pages[m][:])
 
-        for i in range(len(PIECES)):
-            write_piece(i, *make_z(i))
+        fetch_d(0, "picked2")
+        second = second_term(0)
+        fetch_d(1, "picked0")
+        fetch_old(2, "d2")
+        fetch_old(3, "d3")
+        z_q = make_z(0, second)
+        w3_q = [quantise_w3(half) for half in range(2)]
+        write_piece(0, *z_q)
+        write_piece(1, *make_z(1, second_term(1)))

@@ -148,7 +148,8 @@ def tile_picked_twhcrossbpaget_none_p_kernel(tc, x_words, x_scales, w1, w2, gn, 
             cols = slice(half * 2 * P, (half + 1) * 2 * P)
             rounded = keep.tile([P, 2 * P * PACK], BF16, name=f"w3_bf{half}", align_bytes=64)
             nc.vector.tensor_copy(
-                rounded[:].rearrange("p (c j) -> p c j", j=PACK), w3_raw[:, :, cols].rearrange("p j c -> p c j")
+                rounded[:].rearrange("p (c e j) -> p c j e", e=2, j=PACK),
+                w3_raw[:, :, cols].rearrange("p j (c e) -> p c j e", e=2),
             )
             return quantise(rounded[:], f"w3_q{half}")
 
@@ -168,9 +169,9 @@ def tile_picked_twhcrossbpaget_none_p_kernel(tc, x_words, x_scales, w1, w2, gn, 
                 nc.vector.tensor_tensor(first[:, t, :], y_rows[t][:, lo:hi], d_picked[i][:, t, :], ALU.mult)
             z_bf = keep.tile([P, width * PACK], BF16, name=f"z_bf{i}", align_bytes=64)
             nc.vector.tensor_tensor(
-                z_bf[:].rearrange("p (c e t) -> p c t e", e=4, t=PACK),
-                first[:].rearrange("p t (c e) -> p c t e", e=4),
-                second[:].rearrange("p t (c e) -> p c t e", e=4),
+                z_bf[:].rearrange("p (c e t) -> p c t e", e=2, t=PACK),
+                first[:].rearrange("p t (c e) -> p c t e", e=2),
+                second[:].rearrange("p t (c e) -> p c t e", e=2),
                 ALU.subtract,
             )
             return quantise(z_bf[:], f"z_q{i}")

@@ -87,7 +87,9 @@ def tile_picked_twhcrossbpaget_none_p_kernel(tc, x_words, x_scales, w1, w2, gn, 
 
         def first_product(raw, words, scale_cols, name, leave, casts):
             for half in range(2):
-                rounded = keep.tile([P, 2 * P * PACK], BF16, name=f"{name}_bf{half}", align_bytes=64)
+                rounded = keep.tile(
+                    [P, 2 * P * PACK], BF16, name=f"{name}_bf{half}", tag=f"{name}_bf{half}", align_bytes=64
+                )
                 casts[half](
                     rounded[:].rearrange("p (t m j) -> p m t j", t=2, j=PACK),
                     raw[:].rearrange("p j (m t) -> p m t j", t=PACK)[:, :, 2 * half : 2 * half + 2, :],
@@ -144,14 +146,19 @@ def tile_picked_twhcrossbpaget_none_p_kernel(tc, x_words, x_scales, w1, w2, gn, 
                 nc.scalar.activation(tile[:, t, :], d_rows[t][:].indirect(entries(l_n2, lo, hi)), ACT.Copy)
             d_picked.append(tile)
 
-        def quantise_w3(half):
+        w3_bf = [
+            keep.tile([P, 2 * P * PACK], BF16, name="w3_bf0", align_bytes=64),
+            keep.tile([P, 2 * P * PACK], BF16, name="w3_bf1", tag="w2_bf1", align_bytes=64),
+        ]
+
+        def w3_views(half):
             cols = slice(half * 2 * P, (half + 1) * 2 * P)
-            rounded = keep.tile([P, 2 * P * PACK], BF16, name=f"w3_bf{half}", align_bytes=64)
-            nc.vector.tensor_copy(
-                rounded[:].rearrange("p (c e j) -> p c j e", e=2, j=PACK),
+            return (
+                w3_bf[half][:].rearrange("p (c e j) -> p c j e", e=2, j=PACK),
                 w3_raw[:, :, cols].rearrange("p j (c e) -> p c j e", e=2),
             )
-            return quantise(rounded[:], f"w3_q{half}")
+
+        nc.gpsimd.tensor_scalar(*w3_views(1), 1.0, 0.0, ALU.mult, ALU.add)
 
         def second_term(i):
             lo, hi = PIECES[i]
@@ -176,10 +183,10 @@ def tile_picked_twhcrossbpaget_none_p_kernel(tc, x_words, x_scales, w1, w2, gn, 
             )
             return quantise(z_bf[:], f"z_q{i}")
 
-        def write_piece(i, z_codes, z_scales):
+        def write_piece(i, z_codes, z_scales, row_tiles):
             lo, hi = PIECES[i]
             width = hi - lo
-            for m in range(4):
+            for m in row_tiles:
                 acc = psum.tile([P, S], F32, name="acc")
                 h = acc[:, 0:width]
                 nc.tensor.matmul_mx(
@@ -212,6 +219,9 @@ def tile_picked_twhcrossbpaget_none_p_kernel(tc, x_words, x_scales, w1, w2, gn, 
         fetch_old(2, "d2")
         fetch_old(3, "d3")
         z_q = make_z(0, second)
-        w3_q = [quantise_w3(half) for half in range(2)]
-        write_piece(0, *z_q)
-        write_piece(1, *make_z(1, second_term(1)))
+        nc.vector.tensor_copy(*w3_views(0))
+        w3_q = [quantise(w3_bf[half][:], f"w3_q{half}") for half in range(2)]
+        write_piece(0, *z_q, range(3))
+        z_next = make_z(1, second_term(1))
+        write_piece(0, *z_q, range(3, 4))
+        write_piece(1, *z_next, range(4))

from contextlib import ExitStack

import concourse.mybir as mybir

K, T, S, N, H, U = 512, 2048, 512, 512, 512, 1024
FLOPS = 2 * S * (K * H + K * H + H * N)

F32 = mybir.dt.float32
BF16 = mybir.dt.bfloat16
I32 = mybir.dt.int32
U32 = mybir.dt.uint32
U16 = mybir.dt.uint16
U8 = mybir.dt.uint8
FP8X4 = mybir.dt.float8_e4m3fn_x4
ALU = mybir.AluOpType
ACT = mybir.ActivationFunctionType

P = 128
PACK = 4
PIECES = ((0, 256), (256, 512))


def tile_picked_twhcrossbpaget_none_p_kernel(tc, x_words, x_scales, w1, w2, gn, w3, mem, offs, hz, n1, n2, n3, out):
    nc = tc.nc
    with ExitStack() as ctx:
        lists = ctx.enter_context(tc.tile_pool(name="lists", bufs=1))
        keep = ctx.enter_context(tc.tile_pool(name="keep", bufs=1))
        shared = ctx.enter_context(tc.tile_pool(name="shared", bufs=1))
        psum = ctx.enter_context(tc.psum_pool(name="psum", bufs=8))

        def load_list(src, name):
            tile = lists.tile([P, S // 16], U16, name=name)
            nc.sync.dma_start(tile[:], src)
            return tile

        def entries(tile, lo, hi):
            return tile[:, lo // 16 : hi // 16]

        gn_rows = keep.tile([P, PACK], F32, name="gn_rows")
        nc.sync.dma_start(gn_rows[:], gn.rearrange("(p t) o -> p (t o)", t=PACK))
        gain = keep.tile([P, PACK], F32, name="gain")
        nc.scalar.activation(gain[:], gn_rows[:], ACT.Copy, scale=0.75)
        l_offs = load_list(offs, "l_offs")
        l_hz = load_list(hz, "l_hz")
        l_n3 = load_list(n3, "l_n3")
        l_n1 = load_list(n1, "l_n1")
        l_n2 = load_list(n2, "l_n2")
        scale_table = shared.tile([P, T], U8, name="scale_table", align_bytes=64, offset=16384 + 3072)
        nc.vector.memset(scale_table[:].bitcast(I32), 0)
        nc.sync.dma_start(scale_table[0:P:8, :].bitcast(I32), x_scales[0].bitcast(I32))
        word_table = shared.tile([P, T], U32, name="word_table", offset=0)
        nc.sync.dma_start(word_table[:].bitcast(I32), x_words[0].rearrange("p n t -> p (n t)").bitcast(I32))

        def load_weight(w, name, offset):
            raw = shared.tile([P, PACK, 512], F32, name=name, offset=offset)
            nc.sync.dma_start(raw[:], w.rearrange("(p j) c -> p j c", j=PACK))
            return raw

        def load_page(m, tile):
            nc.sync.dma_start(tile[:], mem[m * P : (m + 1) * P, :])
            return tile

        w1_raw = load_weight(w1, "w1_raw", 8192)
        pages = [load_page(0, keep.tile([P, U], F32, name="page0"))]

        picked_scales = keep.tile([P, 2 * S], U8, name="picked_scales", align_bytes=64)
        nc.vector.tensor_copy(picked_scales[:, 0:S], scale_table[:].indirect(l_offs[:]))
        nc.vector.tensor_copy(picked_scales[:, S : 2 * S], scale_table[:].indirect(l_hz[:]))
        placed_scales = keep.tile([P, 2 * S], U8, name="placed_scales", align_bytes=64)
        nc.vector.memset(placed_scales[:].bitcast(I32), 0)
        for r in range(4):
            nc.sync.dma_start(placed_scales[r:P:32, :].bitcast(I32), picked_scales[8 * r : P : 32, :].bitcast(I32))
        pages.append(load_page(1, shared.tile([P, U], F32, name="page1", offset=16384)))
        w2_raw = load_weight(w2, "w2_raw", 20480)
        words_offs = keep.tile([P, S], U32, name="words_offs", align_bytes=64)
        nc.vector.tensor_copy(words_offs[:], word_table[:].indirect(l_offs[:]))
        words_hz = keep.tile([P, S], U32, name="words_hz", align_bytes=64)
        nc.vector.tensor_copy(words_hz[:], word_table[:].indirect(l_hz[:]))
        w3_raw = load_weight(w3, "w3_raw", 0)

        def quantise(values, name):
            width = values.shape[1] // PACK
            codes = keep.tile([P, width], U32, name=name + "_codes", align_bytes=64)
            scales = keep.tile([P, width], U8, name=name + "_scales", align_bytes=64)
            nc.vector.quantize_mx(out=codes[:].bitcast(FP8X4), scales=scales[:], in_=values)
            return codes, scales

        def first_product(raw, words, scale_cols, name, leave, casts):
            for half in range(2):
                rounded = keep.tile(
                    [P, 2 * P * PACK], BF16, name=f"{name}_bf{half}", tag=f"{name}_bf{half}", align_bytes=64
                )
                casts[half](
                    rounded[:].rearrange("p (t m j) -> p m t j", t=2, j=PACK),
                    raw[:].rearrange("p j (m t) -> p m t j", t=PACK)[:, :, 2 * half : 2 * half + 2, :],
                )
                codes, scales = quantise(rounded[:], f"{name}_q{half}")
                for u in range(2):
                    acc = psum.tile([P, S], F32, name="acc")
                    nc.tensor.matmul_mx(
                        out=acc[:],
                        lhsT=codes[:, u * P : (u + 1) * P].bitcast(FP8X4),
                        lhsT_scale=scales[:, u * P : (u + 1) * P],
                        rhs=words[:].bitcast(FP8X4),
                        rhs_scale=placed_scales[:, scale_cols],
                        start=True,
                        stop=True,
                    )
                    leave(2 * half + u, acc)

        old = []

        def fetch_old(m, tag):
            tile = keep.tile([P, S], F32, name=f"old{m}", tag=tag)
            nc.scalar.activation(tile[:], pages[m][:].indirect(l_n3[:]), ACT.Copy)
            old.append(tile)

        y_rows, d_rows, d_banks = [], [], []
        y_picked = [keep.tile([P, PACK, hi - lo], F32, name=f"y_picked{i}", tag=f"picked{i}") for i, (lo, hi) in enumerate(PIECES)]
        d_picked = []

        def leave_y(t, acc):
            row = keep.tile([P, S], F32, name=f"y{t}")
            nc.vector.tensor_scalar(row[:], acc[:], gain[:, t : t + 1], None, ALU.mult)
            y_rows.append(row)
            for i, (lo, hi) in enumerate(PIECES):
                nc.scalar.activation(y_picked[i][:, t, :], row[:].indirect(entries(l_n1, lo, hi)), ACT.Copy)

        def leave_d(t, acc):
            row = keep.tile([P, S], F32, name=f"d{t}", tag=f"d{t}")
            nc.vector.tensor_copy(row[:], acc[:])
            d_rows.append(row)
            d_banks.append(acc)

        first_product(w1_raw, words_offs, slice(0, S), "w1", leave_y, (nc.vector.tensor_copy, nc.scalar.copy))
        fetch_old(0, "old0")
        fetch_old(1, "old1")
        for m in range(2, 4):
            pages.append(load_page(m, shared.tile([P, U], F32, name=f"page{m}", offset=8192 + (m - 2) * U * 4)))
        first_product(w2_raw, words_hz, slice(S, 2 * S), "w2", leave_d, (nc.vector.tensor_copy, nc.vector.tensor_copy))

        def fetch_d(i, tag):
            lo, hi = PIECES[i]
            tile = keep.tile([P, PACK, hi - lo], F32, name=f"d_picked{i}", tag=tag)
            for t in range(PACK):
                nc.scalar.activation(tile[:, t, :], d_rows[t][:].indirect(entries(l_n2, lo, hi)), ACT.Copy)
            d_picked.append(tile)

        w3_bf = [
            keep.tile([P, 2 * P * PACK], BF16, name="w3_bf0", align_bytes=64),
            keep.tile([P, 2 * P * PACK], BF16, name="w3_bf1", tag="w2_bf1", align_bytes=64),
        ]

        def w3_views(half):
            cols = slice(half * 2 * P, (half + 1) * 2 * P)
            return (
                w3_bf[half][:].rearrange("p (c e j) -> p c j e", e=2, j=PACK),
                w3_raw[:, :, cols].rearrange("p j (c e) -> p c j e", e=2),
            )

        nc.gpsimd.tensor_scalar(*w3_views(1), 1.0, 0.0, ALU.mult, ALU.add)

        def second_term(i):
            lo, hi = PIECES[i]
            width = hi - lo
            second = keep.tile([P, PACK, width], F32, name=f"second{i}", tag=f"product{(i + 1) % 2}")
            for t in range(PACK):
                nc.vector.tensor_tensor(second[:, t, :], d_banks[t][:, lo:hi], y_picked[i][:, t, :], ALU.mult)
            return second

        def make_z(i, second):
            lo, hi = PIECES[i]
            width = hi - lo
            first = keep.tile([P, PACK, width], F32, name=f"first{i}", tag=f"product{i % 2}")
            for t in range(PACK):
                nc.vector.tensor_tensor(first[:, t, :], y_rows[t][:, lo:hi], d_picked[i][:, t, :], ALU.mult)
            z_bf = keep.tile([P, width * PACK], BF16, name=f"z_bf{i}", align_bytes=64)
            nc.vector.tensor_tensor(
                z_bf[:].rearrange("p (c e t) -> p c t e", e=2, t=PACK),
                first[:].rearrange("p t (c e) -> p c t e", e=2),
                second[:].rearrange("p t (c e) -> p c t e", e=2),
                ALU.subtract,
            )
            return quantise(z_bf[:], f"z_q{i}")

        def write_piece(i, z_codes, z_scales, row_tiles):
            lo, hi = PIECES[i]
            width = hi - lo
            for m in row_tiles:
                acc = psum.tile([P, S], F32, name="acc")
                h = acc[:, 0:width]
                nc.tensor.matmul_mx(
                    out=h,
                    lhsT=w3_q[m // 2][0][:, m % 2 * P : (m % 2 + 1) * P].bitcast(FP8X4),
                    lhsT_scale=w3_q[m // 2][1][:, m % 2 * P : (m % 2 + 1) * P],
                    rhs=z_codes[:].bitcast(FP8X4),
                    rhs_scale=z_scales[:],
                    start=True,
                    stop=True,
                )
                gap = keep.tile([P, width], F32, name=f"gap{i}_{m}")
                half_tanh = keep.tile([P, width], F32, name=f"tanh{i}_{m}")
                if m < 2:
                    nc.vector.tensor_tensor(gap[:], h, old[m][:, lo:hi], ALU.subtract)
                nc.scalar.activation(half_tanh[:], h, ACT.Tanh, scale=0.5)
                if m >= 2:
                    nc.vector.tensor_tensor(gap[:], h, old[m][:, lo:hi], ALU.subtract)
                step = keep.tile([P, width], F32, name=f"step{i}_{m}")
                nc.vector.scalar_tensor_tensor(step[:], half_tanh[:], 1.0, gap[:], ALU.add, ALU.mult)
                new = keep.tile([P, width], F32, name=f"new{i}_{m}")
                nc.vector.scalar_tensor_tensor(new[:], step[:], 0.5, old[m][:, lo:hi], ALU.mult, ALU.add)
                nc.scalar.activation(pages[m][:].indirect(entries(l_n3, lo, hi)), new[:], ACT.Copy)
                if hi == S:
                    nc.sync.dma_start(out[m * P : (m + 1) * P, :], pages[m][:])

        fetch_d(0, "picked2")
        second = second_term(0)
        fetch_d(1, "picked0")
        fetch_old(2, "d2")
        fetch_old(3, "d3")
        z_q = make_z(0, second)
        nc.vector.tensor_copy(*w3_views(0))
        w3_q = [quantise(w3_bf[half][:], f"w3_q{half}") for half in range(2)]
        write_piece(0, *z_q, range(3))
        z_next = make_z(1, second_term(1))
        write_piece(0, *z_q, range(3, 4))
        write_piece(1, *z_next, range(4))
